import numpy as np
import ml_dtypes


def mxq(x, axis, fmt="e4m3"):
    dtype, down = {"e4m3": (ml_dtypes.float8_e4m3fn, 7), "e5m2": (ml_dtypes.float8_e5m2, 14)}[fmt]
    v = np.moveaxis(np.asarray(x, np.float32).astype(ml_dtypes.bfloat16).astype(np.float64), axis, -1)
    blocks = v.reshape(v.shape[:-1] + (-1, 32))
    amax = np.abs(blocks).max(-1, keepdims=True)
    byte = np.maximum(np.where(amax > 0, np.frexp(amax)[1] - 1 + 127, 0) - down, 1)
    scale = np.exp2(byte - 127.0)
    codes = (blocks / scale).astype(np.float32).astype(dtype).astype(np.float64)
    return np.moveaxis((codes * scale).reshape(v.shape), -1, axis)


WIDE = False


def mx_kscale(k):
    if not WIDE:
        return np.ones(k)
    levels = np.array([10, -10, 5, -5, 0])
    if k % 512:
        return np.exp2(np.random.permutation(np.resize(levels, k // 32))).repeat(32)
    a = np.empty((k // 512, 16))
    for p in range(k // 512):
        a[p, :8] = np.random.permutation(np.resize(levels, 8))
        for g in range(8):
            far = levels[np.abs(levels - a[p, g]) >= 10]
            a[p, g + 8] = far[np.random.randint(len(far))]
    return np.exp2(a.ravel()).repeat(32)


def f64(x):
    return np.asarray(x).astype(np.float64)


def striped(idx):
    return np.tile(idx.reshape(-1, 16).T, (8, 1)).astype(np.uint16)


def unstriped(offs):
    return offs[:16].T.reshape(-1).astype(np.int64)


E2M1 = np.array([0.0, 0.5, 1.0, 1.5, 2.0, 3.0, 4.0, 6.0, -0.0, -0.5, -1.0, -1.5, -2.0, -3.0, -4.0, -6.0])


def pack_weight(w, fmt):
    k, n = w.shape
    w = f64(np.asarray(w, np.float32).astype(ml_dtypes.bfloat16)).reshape(k // 32, 32, n)
    amax = np.abs(w).max(1)
    if fmt == "e4m3":
        byte = np.frexp(amax)[1] - 1 + 127 - 7
    else:
        mant, ex = np.frexp(amax / 6.0)
        byte = np.where(mant > 0.5, ex, ex - 1) + 127
    byte = np.clip(np.where(amax > 0, byte, 1), 1, 254)
    scaled = (w * np.exp2(127.0 - byte)[:, None, :]).reshape(k, n).astype(np.float32)
    by_word = np.ascontiguousarray(scaled.reshape(k // 512, 128, 4, n).transpose(0, 1, 3, 2))
    if fmt == "e4m3":
        words = by_word.astype(ml_dtypes.float8_e4m3fn).view(np.uint8)
    else:
        c = by_word.astype(ml_dtypes.float4_e2m1fn).view(np.uint8) & 0xF
        words = (c[..., 0::2] | (c[..., 1::2] << 4)).reshape(k // 512, 128, 2 * n)
    return np.ascontiguousarray(words), np.ascontiguousarray(byte.astype(np.uint8).reshape(k // 512, 16, n))


def unpack_weight(words, scales, fmt):
    g, _, n = scales.shape
    words = np.ascontiguousarray(words).reshape(g, 128, n, -1)
    if fmt == "e4m3":
        vals = words.view(ml_dtypes.float8_e4m3fn).astype(np.float64)
    else:
        nib = np.empty((g, 128, n, 4), np.uint8)
        nib[..., 0::2] = words & 0xF
        nib[..., 1::2] = words >> 4
        vals = E2M1[nib]
    vals = vals * np.repeat(np.exp2(scales.astype(np.float64) - 127.0), 8, axis=1)[..., None]
    return vals.transpose(0, 1, 3, 2).reshape(g * 512, n)


def silu(v):
    return v / (1.0 + np.exp(-np.maximum(v, -700.0)))


K, T, E, C, N = 512, 384, 6, 128, 512


def by_expert(wq, xq):
    return np.concatenate([wq[e].T @ xq[:, e * C:(e + 1) * C] for e in range(E)], axis=1)


def setup_inputs():
    n = np.random.standard_normal
    s = mx_kscale(K)[:, None]
    first = np.random.permutation(np.repeat(np.arange(E), T // E))
    second = (first + 1 + np.random.permutation(np.repeat(np.arange(E - 1), -(-T // (E - 1)))[:T])) % E
    while np.bincount(second, minlength=E).max() != T // E:
        load = np.bincount(second, minlength=E); hi, lo = int(load.argmax()), int(load.argmin())
        t = np.flatnonzero((second == hi) & (first != lo))[0]; second[t] = lo
    slot_token = np.empty(E * C, np.int64); pos = np.empty((2, T), np.int64); fill = np.zeros(E, np.int64)
    place = np.stack([np.random.permutation(C) for _ in range(E)])
    for r, deal in enumerate((first, second)):
        for t in np.random.permutation(T):
            e = deal[t]; j = e * C + place[e, fill[e]]; fill[e] += 1; slot_token[j] = t; pos[r, t] = j
    g = np.random.uniform(0.2, 0.8, T)
    w = [pack_weight(m, "e2m1") for m in n((E + 1, K, N)) / np.sqrt(K) / s[None]]
    return {
        "xT": (n((K, T)) * s).astype(np.float32),
        "w_words": np.stack([m[0] for m in w]),
        "w_scales": np.stack([m[1] for m in w]),
        "b": (0.3 * n((N, E + 1))).astype(np.float32),
        "gate": np.stack([np.tile(g, (N, 1)), np.tile(1.0 - g, (N, 1))]).astype(np.float32),
        "offs": striped(slot_token),
        "pos1": striped(pos[0]),
        "pos2": striped(pos[1]),
    }


def reference(xT, w_words, w_scales, b, gate, offs, pos1, pos2):
    idx = unstriped(offs)
    w = np.stack([unpack_weight(w_words[e], w_scales[e], "e2m1") for e in range(E + 1)])
    wq = w
    xs = mxq(f64(xT), 0, "e4m3")
    ys = silu((wq[E].T @ xs) + f64(b)[:, E:])
    xq = mxq(f64(xT)[:, idx], 0, "e4m3")
    y = by_expert(w, xq)
    y = silu(y + np.repeat(f64(b)[:, :E], C, axis=1))
    return ys + f64(gate[0]) * y[:, unstriped(pos1)] + f64(gate[1]) * y[:, unstriped(pos2)]

@@ -1,0 +1,187 @@
+import concourse.mybir as mybir
+from contextlib import ExitStack
+
+K, T, E, C, N = 512, 384, 6, 128, 512
+S = E * C
+P = 128
+M_TILES = N // P
+
+F32 = mybir.dt.float32
+BF16 = mybir.dt.bfloat16
+I32 = mybir.dt.int32
+U32 = mybir.dt.uint32
+U16 = mybir.dt.uint16
+U8 = mybir.dt.uint8
+FP8X4 = mybir.dt.float8_e4m3fn_x4
+FP4X4 = mybir.dt.float4_e2m1fn_x4
+
+MULT = mybir.AluOpType.mult
+ADD = mybir.AluOpType.add
+SILU = mybir.ActivationFunctionType.Silu
+COPY = mybir.ActivationFunctionType.Copy
+
+FLOPS = 2 * K * N * (S + T)
+BYTES = 4 * K * T + (E + 1) * (K * N // 2 + K * N // 32) + 4 * N * (E + 1) + 2 * 4 * T + 2 * 128 * (48 + 24 + 24) + 4 * N * T
+
+WINDOW = 512
+
+
+def tile_moe_shr_lin_silu_kernel(tc, xT, w_words, w_scales, b, gate, offs, pos1, pos2, out):
+    nc = tc.nc
+    with ExitStack() as ctx:
+        lists = ctx.enter_context(tc.tile_pool(name="lists", bufs=1))
+        keep = ctx.enter_context(tc.tile_pool(name="keep", bufs=1))
+        psum = ctx.enter_context(tc.psum_pool(name="psum", bufs=8))
+
+        offs_t = lists.tile([P, S // 16], U16, name="offs_t")
+        pos1_t = lists.tile([P, T // 16], U16, name="pos1_t")
+        pos2_t = lists.tile([P, T // 16], U16, name="pos2_t")
+
+        raw = [keep.tile([P, 2, T], F32, name=f"raw{u}") for u in range(2)]
+        pairs = [keep.tile([P, 2 * WINDOW], BF16, name=f"pairs{u}", align_bytes=64) for u in range(2)]
+        scales_w = keep.tile([P, (E + 1) * N], U8, name="scales_w", align_bytes=64)
+        bias = keep.tile([P, M_TILES, E + 1], F32, name="bias")
+        dummy = keep.tile([P, 1], F32, name="dummy")
+        gates = [keep.tile([P, 2, T], F32, name=f"gates{m}") for m in range(M_TILES)]
+
+        x_rows = xT.rearrange("(p u e) t -> p u e t", u=2, e=2)
+        nc.sync.dma_start(raw[0][:], x_rows[:, 0])
+        nc.sync.dma_start(offs_t[:], offs)
+        nc.sync.dma_start(raw[1][:], x_rows[:, 1])
+
+        nc.vector.memset(scales_w[:].bitcast(I32), 0)
+        nc.gpsimd.memset(dummy[:], 0.0)
+        nc.scalar.activation(dummy[:], dummy[:], SILU)
+        for u in range(2):
+            nc.gpsimd.memset(pairs[u][:, 2 * T :], 0.0)
+
+        w_scales_i = w_scales.bitcast(I32)
+        scales_i = scales_w[:].bitcast(I32).rearrange("p (e c) -> p e c", e=E + 1)
+        w_i = w_words.bitcast(I32)
+        words = {}
+        for e0, e1 in ((0, 2), (2, 6), (6, 7)):
+            tile = keep.tile([P, (e1 - e0) * 2 * N], U8, name=f"words{e0}", align_bytes=64)
+            nc.sync.dma_start(
+                tile[:].bitcast(I32).rearrange("p (e c) -> p e c", e=e1 - e0),
+                w_i[e0:e1].rearrange("e a p c -> p (e a) c"),
+            )
+            for e in range(e0, e1):
+                words[e] = tile[:, (e - e0) * 2 * N : (e - e0 + 1) * 2 * N]
+            if e0 == 0:
+                for q in range(4):
+                    nc.sync.dma_start(
+                        scales_i[32 * q : 32 * q + 4],
+                        w_scales_i[:, 0, 4 * q : 4 * q + 4, :].rearrange("e q c -> q e c"),
+                    )
+                nc.sync.dma_start(bias[:], b.rearrange("(m p) e -> p m e", p=P))
+        nc.sync.dma_start(pos1_t[:], pos1)
+        nc.sync.dma_start(pos2_t[:], pos2)
+        for m in range(M_TILES):
+            nc.sync.dma_start(gates[m][:], gate[:, m * P : (m + 1) * P, :].rearrange("r p t -> p r t"))
+
+        def cast(engine_copy, u, t0, t1):
+            engine_copy(
+                pairs[u][:, 2 * t0 : 2 * t1].rearrange("p (t e) -> p t e", e=2),
+                raw[u][:, :, t0:t1].rearrange("p e t -> p t e"),
+            )
+
+        cast(nc.vector.tensor_copy, 0, 0, 256)
+        cast(nc.scalar.copy, 0, 256, T)
+        cast(nc.scalar.copy, 1, 0, T)
+
+        windows = [pairs[u][:].bitcast(U32) for u in range(2)]
+
+        def lhsT(e, m):
+            return dict(
+                lhsT=words[e][:, 2 * m * P : 2 * (m + 1) * P].bitcast(FP4X4),
+                lhsT_scale=scales_w[:, e * N + m * P : e * N + (m + 1) * P],
+            )
+
+        shared = keep.tile([P, T, 4], BF16, name="shared", align_bytes=64)
+        for u in range(2):
+            nc.scalar.copy(shared[:, :, 2 * u : 2 * u + 2], raw[u][:].rearrange("p e t -> p t e"))
+
+        y = [keep.tile([P, S], F32, name=f"y{m}") for m in range(M_TILES)]
+        ys = [keep.tile([P, T], F32, name=f"ys{m}") for m in range(M_TILES)]
+        W = 2 * C
+        picked = [keep.tile([P, 4 * W], BF16, name=f"picked{g}", align_bytes=64) for g in range(3)]
+        codes = [keep.tile([P, W], U32, name=f"codes{g}", align_bytes=64) for g in range(3)]
+        scales = [keep.tile([P, W], U8, name=f"scales{g}", align_bytes=64) for g in range(3)]
+
+        def pick(g, u):
+            slots = picked[g][:].bitcast(U32).rearrange("p (s u) -> p s u", u=2)
+            nc.vector.tensor_copy(slots[:, :, u], windows[u].indirect(offs_t[:, g * W // 16 : (g + 1) * W // 16]))
+
+        def quantise(g):
+            nc.vector.quantize_mx(out=codes[g][:].bitcast(FP8X4), scales=scales[g][:], in_=picked[g][:])
+
+        for g, u in ((0, 0), (1, 0), (0, 1), (0, 2), (2, 0), (1, 1), (1, 2), (2, 1), (2, 2)):
+            if u < 2:
+                pick(g, u)
+            else:
+                quantise(g)
+
+        shared_codes = keep.tile([P, T], U32, name="shared_codes", align_bytes=64)
+        shared_scales = keep.tile([P, T], U8, name="shared_scales", align_bytes=64)
+        for t0, t1 in ((0, 256), (256, T)):
+            nc.vector.quantize_mx(
+                out=shared_codes[:, t0:t1].bitcast(FP8X4),
+                scales=shared_scales[:, t0:t1],
+                in_=shared[:, t0:t1].rearrange("p t j -> p (t j)"),
+            )
+
+        for m in range(M_TILES):
+            for g in range(3):
+                sums = psum.tile([P, 2, C], F32, name="sums")
+                for h in range(2):
+                    nc.tensor.matmul_mx(
+                        out=sums[:, h, :],
+                        rhs=codes[g][:, h * C : (h + 1) * C].bitcast(FP8X4),
+                        rhs_scale=scales[g][:, h * C : (h + 1) * C],
+                        start=True,
+                        stop=True,
+                        **lhsT(2 * g + h, m),
+                    )
+                for h in range(2):
+                    e = 2 * g + h
+                    nc.scalar.activation(y[m][:, e * C : (e + 1) * C], sums[:, h, :], SILU, bias=bias[:, m, e : e + 1])
+            sums = psum.tile([P, T], F32, name="sums")
+            for t0, t1 in ((0, 256), (256, T)):
+                nc.tensor.matmul_mx(
+                    out=sums[:, t0:t1],
+                    rhs=shared_codes[:, t0:t1].bitcast(FP8X4),
+                    rhs_scale=shared_scales[:, t0:t1],
+                    start=True,
+                    stop=True,
+                    **lhsT(E, m),
+                )
+            nc.scalar.activation(ys[m][:], sums[:], SILU, bias=bias[:, m, E : E + 1])
+
+        first = [keep.tile([P, T], F32, name=f"first{m}") for m in range(M_TILES)]
+        second = [keep.tile([P, T], F32, name=f"second{m}") for m in range(M_TILES)]
+        part = [keep.tile([P, T], F32, name=f"part{m}") for m in range(M_TILES)]
+        total = [keep.tile([P, T], F32, name=f"total{m}") for m in range(M_TILES)]
+
+        def gather(to, m, listed, r, t0, t1):
+            nc.vector.tensor_tensor(
+                to[m][:, t0:t1], y[m][:].indirect(listed[:, t0 // 16 : t1 // 16]), gates[m][:, r, t0:t1], MULT
+            )
+
+        def finish(m, t0, t1):
+            nc.vector.tensor_tensor(total[m][:, t0:t1], part[m][:, t0:t1], second[m][:, t0:t1], ADD)
+            nc.sync.dma_start(out[m * P : (m + 1) * P, t0:t1], total[m][:, t0:t1])
+
+        H = T // 2
+        for m in range(M_TILES):
+            gather(first, m, pos1_t, 0, 0, T)
+            if m > 0:
+                finish(m - 1, 0, T)
+            if m == M_TILES - 1:
+                gather(second, m, pos2_t, 1, 0, H)
+            nc.vector.tensor_tensor(part[m][:], ys[m][:], first[m][:], ADD)
+            if m < M_TILES - 1:
+                gather(second, m, pos2_t, 1, 0, T)
+            else:
+                gather(second, m, pos2_t, 1, H, T)
+        finish(M_TILES - 1, 0, H)
+        finish(M_TILES - 1, H, T)

@@ -37,23 +37,25 @@ def tile_moe_shr_lin_silu_kernel(tc, xT, w_words, w_scales, b, gate, offs, pos1,
         pos1_t = lists.tile([P, T // 16], U16, name="pos1_t")
         pos2_t = lists.tile([P, T // 16], U16, name="pos2_t")
 
-        raw = [keep.tile([P, 2, T], F32, name=f"raw{u}") for u in range(2)]
+        raw = keep.tile([P, 4, T], F32, name="raw")
         pairs = [keep.tile([P, 2 * WINDOW], BF16, name=f"pairs{u}", align_bytes=64) for u in range(2)]
+        rows = keep.tile([P, 4, WINDOW], BF16, name="rows", align_bytes=64)
         scales_w = keep.tile([P, (E + 1) * N], U8, name="scales_w", align_bytes=64)
         bias = keep.tile([P, M_TILES, E + 1], F32, name="bias")
         dummy = keep.tile([P, 1], F32, name="dummy")
         gates = [keep.tile([P, 2, T], F32, name=f"gates{m}") for m in range(M_TILES)]
 
-        x_rows = xT.rearrange("(p u e) t -> p u e t", u=2, e=2)
-        nc.sync.dma_start(raw[0][:], x_rows[:, 0])
+        x_rows = xT.rearrange("(p j) t -> p j t", j=4)
+        nc.sync.dma_start(raw[:, 0:2], x_rows[:, 0:2])
         nc.sync.dma_start(offs_t[:], offs)
-        nc.sync.dma_start(raw[1][:], x_rows[:, 1])
+        nc.sync.dma_start(raw[:, 2:4], x_rows[:, 2:4])
 
         nc.vector.memset(scales_w[:].bitcast(I32), 0)
         nc.gpsimd.memset(dummy[:], 0.0)
         nc.scalar.activation(dummy[:], dummy[:], SILU)
         for u in range(2):
             nc.gpsimd.memset(pairs[u][:, 2 * T :], 0.0)
+        nc.gpsimd.memset(rows[:, :, T:], 0.0)
 
         w_scales_i = w_scales.bitcast(I32)
         scales_i = scales_w[:].bitcast(I32).rearrange("p (e c) -> p e c", e=E + 1)
@@ -82,14 +84,8 @@ def tile_moe_shr_lin_silu_kernel(tc, xT, w_words, w_scales, b, gate, offs, pos1,
         def cast(engine_copy, u, t0, t1):
             engine_copy(
                 pairs[u][:, 2 * t0 : 2 * t1].rearrange("p (t e) -> p t e", e=2),
-                raw[u][:, :, t0:t1].rearrange("p e t -> p t e"),
+                raw[:, 2 * u : 2 * u + 2, t0:t1].rearrange("p e t -> p t e"),
             )
-
-        cast(nc.vector.tensor_copy, 0, 0, 256)
-        cast(nc.scalar.copy, 0, 256, T)
-        cast(nc.scalar.copy, 1, 0, T)
-
-        windows = [pairs[u][:].bitcast(U32) for u in range(2)]
 
         def lhsT(e, m):
             return dict(
@@ -97,91 +93,126 @@ def tile_moe_shr_lin_silu_kernel(tc, xT, w_words, w_scales, b, gate, offs, pos1,
                 lhsT_scale=scales_w[:, e * N + m * P : e * N + (m + 1) * P],
             )
 
-        shared = keep.tile([P, T, 4], BF16, name="shared", align_bytes=64)
-        for u in range(2):
-            nc.scalar.copy(shared[:, :, 2 * u : 2 * u + 2], raw[u][:].rearrange("p e t -> p t e"))
+        windows = [pairs[u][:].bitcast(U32) for u in range(2)]
+        spans = ((0, 5 * C), (5 * C, S), (S, S + T))
+        picked = [keep.tile([P, s1 - s0, 4], BF16, name=f"picked{s0}", align_bytes=64) for s0, s1 in spans]
+        codes = [keep.tile([P, s1 - s0], U32, name=f"codes{s0}", align_bytes=64) for s0, s1 in spans]
+        scales = [keep.tile([P, s1 - s0], U8, name=f"scales{s0}", align_bytes=64) for s0, s1 in spans]
+        CUTS = ((0, 384), (384, 640))
+        planes = [keep.tile([P, 2, 2 * (s1 - s0)], BF16, name=f"planes{s0}", align_bytes=64) for s0, s1 in CUTS]
+
+        def pick_pairs(i, u):
+            s0, s1 = CUTS[i]
+            nc.vector.tensor_copy(planes[i][:, u].bitcast(U32), windows[u].indirect(offs_t[:, s0 // 16 : s1 // 16]))
+
+        def interleave(i):
+            s0, s1 = CUTS[i]
+            nc.vector.tensor_copy(
+                picked[0][:, s0:s1].rearrange("p s j -> p (s j)").bitcast(I32).rearrange("p (s u) -> p s u", u=2),
+                planes[i][:].rearrange("p u c -> p (u c)").bitcast(I32).rearrange("p (u s) -> p s u", u=2),
+            )
+
+        def pick_row(e, j):
+            nc.scalar.activation(
+                picked[1][:, :, j],
+                rows[:, j].indirect(offs_t[:, e * C // 16 : (e + 1) * C // 16]),
+                COPY,
+            )
+
+        def quantise(i, s0, s1):
+            nc.vector.quantize_mx(
+                out=codes[i][:, s0:s1].bitcast(FP8X4),
+                scales=scales[i][:, s0:s1],
+                in_=picked[i][:, s0:s1].rearrange("p s j -> p (s j)"),
+            )
+
+        cast(nc.vector.tensor_copy, 0, 0, 256)
+        cast(nc.scalar.copy, 0, 256, T)
+        cast(nc.scalar.copy, 1, 0, T)
+        nc.scalar.copy(rows[:, :, 0:T], raw[:])
+        for i in range(2):
+            pick_pairs(i, 0)
+        for j in range(4):
+            pick_row(5, j)
+        for t0, t1 in ((0, 128), (128, 256), (256, T)):
+            nc.gpsimd.tensor_scalar(
+                picked[2][:, t0:t1], raw[:, :, t0:t1].rearrange("p j t -> p t j"), 1.0, 0.0, MULT, ADD
+            )
+        for i in range(2):
+            pick_pairs(i, 1)
+        for i in range(2):
+            interleave(i)
+        for i, s0, s1 in ((0, 0, 256), (0, 256, 512), (0, 512, 640), (1, 0, 128), (2, 0, 256), (2, 256, 384)):
+            quantise(i, s0, s1)
 
         y = [keep.tile([P, S], F32, name=f"y{m}") for m in range(M_TILES)]
-        ys = [keep.tile([P, T], F32, name=f"ys{m}") for m in range(M_TILES)]
-        W = 2 * C
-        picked = [keep.tile([P, 4 * W], BF16, name=f"picked{g}", align_bytes=64) for g in range(3)]
-        codes = [keep.tile([P, W], U32, name=f"codes{g}", align_bytes=64) for g in range(3)]
-        scales = [keep.tile([P, W], U8, name=f"scales{g}", align_bytes=64) for g in range(3)]
+        ys = [keep.tile([P, 2, T], F32, name=f"ys{m}") for m in range(2)]
 
-        def pick(g, u):
-            slots = picked[g][:].bitcast(U32).rearrange("p (s u) -> p s u", u=2)
-            nc.vector.tensor_copy(slots[:, :, u], windows[u].indirect(offs_t[:, g * W // 16 : (g + 1) * W // 16]))
-
-        def quantise(g):
-            nc.vector.quantize_mx(out=codes[g][:].bitcast(FP8X4), scales=scales[g][:], in_=picked[g][:])
-
-        for g, u in ((0, 0), (1, 0), (0, 1), (0, 2), (2, 0), (1, 1), (1, 2), (2, 1), (2, 2)):
-            if u < 2:
-                pick(g, u)
-            else:
-                quantise(g)
-
-        shared_codes = keep.tile([P, T], U32, name="shared_codes", align_bytes=64)
-        shared_scales = keep.tile([P, T], U8, name="shared_scales", align_bytes=64)
-        for t0, t1 in ((0, 256), (256, T)):
-            nc.vector.quantize_mx(
-                out=shared_codes[:, t0:t1].bitcast(FP8X4),
-                scales=shared_scales[:, t0:t1],
-                in_=shared[:, t0:t1].rearrange("p t j -> p (t j)"),
+        def product(sums, e, m, s0, s1):
+            i = [j for j in range(3) if spans[j][0] <= s0 < spans[j][1]][0]
+            s0, s1 = s0 - spans[i][0], s1 - spans[i][0]
+            nc.tensor.matmul_mx(
+                out=sums,
+                rhs=codes[i][:, s0:s1].bitcast(FP8X4),
+                rhs_scale=scales[i][:, s0:s1],
+                start=True,
+                stop=True,
+                **lhsT(e, m),
             )
 
         for m in range(M_TILES):
-            for g in range(3):
+            for e0 in (0, 2, 4):
                 sums = psum.tile([P, 2, C], F32, name="sums")
-                for h in range(2):
-                    nc.tensor.matmul_mx(
-                        out=sums[:, h, :],
-                        rhs=codes[g][:, h * C : (h + 1) * C].bitcast(FP8X4),
-                        rhs_scale=scales[g][:, h * C : (h + 1) * C],
-                        start=True,
-                        stop=True,
-                        **lhsT(2 * g + h, m),
+                for e in (e0, e0 + 1):
+                    product(sums[:, e - e0], e, m, e * C, (e + 1) * C)
+                for e in (e0, e0 + 1):
+                    nc.scalar.activation(
+                        y[m][:, e * C : (e + 1) * C], sums[:, e - e0], SILU, bias=bias[:, m, e : e + 1]
                     )
-                for h in range(2):
-                    e = 2 * g + h
-                    nc.scalar.activation(y[m][:, e * C : (e + 1) * C], sums[:, h, :], SILU, bias=bias[:, m, e : e + 1])
             sums = psum.tile([P, T], F32, name="sums")
             for t0, t1 in ((0, 256), (256, T)):
-                nc.tensor.matmul_mx(
-                    out=sums[:, t0:t1],
-                    rhs=shared_codes[:, t0:t1].bitcast(FP8X4),
-                    rhs_scale=shared_scales[:, t0:t1],
-                    start=True,
-                    stop=True,
-                    **lhsT(E, m),
-                )
-            nc.scalar.activation(ys[m][:], sums[:], SILU, bias=bias[:, m, E : E + 1])
+                product(sums[:, t0:t1], E, m, S + t0, S + t1)
+            nc.scalar.activation(ys[m // 2][:, m % 2], sums[:], SILU, bias=bias[:, m, E : E + 1])
 
-        first = [keep.tile([P, T], F32, name=f"first{m}") for m in range(M_TILES)]
-        second = [keep.tile([P, T], F32, name=f"second{m}") for m in range(M_TILES)]
-        part = [keep.tile([P, T], F32, name=f"part{m}") for m in range(M_TILES)]
-        total = [keep.tile([P, T], F32, name=f"total{m}") for m in range(M_TILES)]
+        first = [keep.tile([P, 2, T], F32, name=f"first{m}") for m in range(2)]
+        second = [keep.tile([P, 2, T], F32, name=f"second{m}") for m in range(2)]
+        part = [keep.tile([P, 2, T], F32, name=f"part{m}") for m in range(2)]
+        total = [keep.tile([P, 2, T], F32, name=f"total{m}") for m in range(2)]
 
-        def gather(to, m, listed, r, t0, t1):
+        def gather(to, m, listed, r, t0=0, t1=T):
             nc.vector.tensor_tensor(
-                to[m][:, t0:t1], y[m][:].indirect(listed[:, t0 // 16 : t1 // 16]), gates[m][:, r, t0:t1], MULT
+                to[m // 2][:, m % 2, t0:t1],
+                y[m][:].indirect(listed[:, t0 // 16 : t1 // 16]),
+                gates[m][:, r, t0:t1],
+                MULT,
             )
 
-        def finish(m, t0, t1):
-            nc.vector.tensor_tensor(total[m][:, t0:t1], part[m][:, t0:t1], second[m][:, t0:t1], ADD)
-            nc.sync.dma_start(out[m * P : (m + 1) * P, t0:t1], total[m][:, t0:t1])
+        def add(to, a, b, m, span, t0=0, t1=T):
+            at = (slice(None), slice(m % 2, m % 2 + span), slice(t0, t1))
+            nc.vector.tensor_tensor(to[m // 2][at], a[m // 2][at], b[m // 2][at], ADD)
 
-        H = T // 2
-        for m in range(M_TILES):
-            gather(first, m, pos1_t, 0, 0, T)
-            if m > 0:
-                finish(m - 1, 0, T)
-            if m == M_TILES - 1:
-                gather(second, m, pos2_t, 1, 0, H)
-            nc.vector.tensor_tensor(part[m][:], ys[m][:], first[m][:], ADD)
-            if m < M_TILES - 1:
-                gather(second, m, pos2_t, 1, 0, T)
-            else:
-                gather(second, m, pos2_t, 1, H, T)
-        finish(M_TILES - 1, 0, H)
-        finish(M_TILES - 1, H, T)
+        def store(m, t0=0, t1=T):
+            nc.sync.dma_start(out[m * P : (m + 1) * P, t0:t1], total[m // 2][:, m % 2, t0:t1])
+
+        gather(first, 0, pos1_t, 0)
+        gather(second, 0, pos2_t, 1)
+        gather(first, 1, pos1_t, 0)
+        gather(second, 1, pos2_t, 1)
+        add(part, ys, first, 0, 2)
+        gather(first, 2, pos1_t, 0)
+        add(total, part, second, 0, 2)
+        store(0)
+        store(1)
+        gather(second, 2, pos2_t, 1)
+        add(part, ys, first, 2, 1)
+        gather(first, 3, pos1_t, 0)
+        add(total, part, second, 2, 1)
+        store(2)
+        LATE = 256
+        gather(second, 3, pos2_t, 1, 0, LATE)
+        add(part, ys, first, 3, 1)
+        gather(second, 3, pos2_t, 1, LATE, T)
+        add(total, part, second, 3, 1, 0, LATE)
+        store(3, 0, LATE)
+        add(total, part, second, 3, 1, LATE, T)
+        store(3, LATE, T)

@@ -39,8 +39,9 @@ def tile_moe_shr_lin_silu_kernel(tc, xT, w_words, w_scales, b, gate, offs, pos1,
 
         raw = keep.tile([P, 4, T], F32, name="raw")
         pairs = [keep.tile([P, 2 * WINDOW], BF16, name=f"pairs{u}", align_bytes=64) for u in range(2)]
-        rows = keep.tile([P, 4, WINDOW], BF16, name="rows", align_bytes=64)
-        scales_w = keep.tile([P, (E + 1) * N], U8, name="scales_w", align_bytes=64)
+        rows = keep.tile([P, 5 * WINDOW], BF16, name="rows", align_bytes=64)
+        words = [keep.tile([P, (E + 1) * N], U8, name=f"words{h}", align_bytes=64) for h in range(2)]
+        scales_w = [keep.tile([P, (E + 1) * N // 2], U8, name=f"scales_w{h}", align_bytes=64) for h in range(2)]
         bias = keep.tile([P, M_TILES, E + 1], F32, name="bias")
         dummy = keep.tile([P, 1], F32, name="dummy")
         gates = [keep.tile([P, 2, T], F32, name=f"gates{m}") for m in range(M_TILES)]
@@ -50,36 +51,42 @@ def tile_moe_shr_lin_silu_kernel(tc, xT, w_words, w_scales, b, gate, offs, pos1,
         nc.sync.dma_start(offs_t[:], offs)
         nc.sync.dma_start(raw[:, 2:4], x_rows[:, 2:4])
 
-        nc.vector.memset(scales_w[:].bitcast(I32), 0)
+        for h in range(2):
+            nc.vector.memset(scales_w[h][:].bitcast(I32), 0)
         nc.gpsimd.memset(dummy[:], 0.0)
         nc.scalar.activation(dummy[:], dummy[:], SILU)
         for u in range(2):
             nc.gpsimd.memset(pairs[u][:, 2 * T :], 0.0)
-        nc.gpsimd.memset(rows[:, :, T:], 0.0)
+        row_of = rows[:].rearrange("p (r t) -> p r t", t=WINDOW)
+        nc.gpsimd.memset(row_of[:, 0:4, T:], 0.0)
+        nc.gpsimd.memset(row_of[:, 4], 0.0)
+        place = (0, 2, 1, 3)
 
         w_scales_i = w_scales.bitcast(I32)
-        scales_i = scales_w[:].bitcast(I32).rearrange("p (e c) -> p e c", e=E + 1)
         w_i = w_words.bitcast(I32)
-        words = {}
-        for e0, e1 in ((0, 2), (2, 6), (6, 7)):
-            tile = keep.tile([P, (e1 - e0) * 2 * N], U8, name=f"words{e0}", align_bytes=64)
+
+        def load_weights(h):
             nc.sync.dma_start(
-                tile[:].bitcast(I32).rearrange("p (e c) -> p e c", e=e1 - e0),
-                w_i[e0:e1].rearrange("e a p c -> p (e a) c"),
+                words[h][:].bitcast(I32).rearrange("p (e c) -> p e c", e=E + 1),
+                w_i[:, 0, :, h * N // 4 : (h + 1) * N // 4].rearrange("e p c -> p e c"),
             )
-            for e in range(e0, e1):
-                words[e] = tile[:, (e - e0) * 2 * N : (e - e0 + 1) * 2 * N]
-            if e0 == 0:
-                for q in range(4):
-                    nc.sync.dma_start(
-                        scales_i[32 * q : 32 * q + 4],
-                        w_scales_i[:, 0, 4 * q : 4 * q + 4, :].rearrange("e q c -> q e c"),
-                    )
-                nc.sync.dma_start(bias[:], b.rearrange("(m p) e -> p m e", p=P))
+            for q in range(4):
+                nc.sync.dma_start(
+                    scales_w[h][:].bitcast(I32).rearrange("p (e c) -> p e c", e=E + 1)[32 * q : 32 * q + 4],
+                    w_scales_i[:, 0, 4 * q : 4 * q + 4, h * N // 8 : (h + 1) * N // 8].rearrange("e q c -> q e c"),
+                )
+
+        def load_gates(m):
+            nc.sync.dma_start(gates[m][:], gate[:, m * P : (m + 1) * P, :].rearrange("r p t -> p r t"))
+
+        load_weights(0)
+        nc.sync.dma_start(bias[:], b.rearrange("(m p) e -> p m e", p=P))
+        load_gates(0)
         nc.sync.dma_start(pos1_t[:], pos1)
         nc.sync.dma_start(pos2_t[:], pos2)
-        for m in range(M_TILES):
-            nc.sync.dma_start(gates[m][:], gate[:, m * P : (m + 1) * P, :].rearrange("r p t -> p r t"))
+        load_weights(1)
+        for m in range(1, M_TILES):
+            load_gates(m)
 
         def cast(engine_copy, u, t0, t1):
             engine_copy(
@@ -88,9 +95,10 @@ def tile_moe_shr_lin_silu_kernel(tc, xT, w_words, w_scales, b, gate, offs, pos1,
             )
 
         def lhsT(e, m):
+            col = e * N // 2 + m % 2 * P
             return dict(
-                lhsT=words[e][:, 2 * m * P : 2 * (m + 1) * P].bitcast(FP4X4),
-                lhsT_scale=scales_w[:, e * N + m * P : e * N + (m + 1) * P],
+                lhsT=words[m // 2][:, 2 * col : 2 * (col + P)].bitcast(FP4X4),
+                lhsT_scale=scales_w[m // 2][:, col : col + P],
             )
 
         windows = [pairs[u][:].bitcast(U32) for u in range(2)]
@@ -115,7 +123,7 @@ def tile_moe_shr_lin_silu_kernel(tc, xT, w_words, w_scales, b, gate, offs, pos1,
         def pick_row(e, j):
             nc.scalar.activation(
                 picked[1][:, :, j],
-                rows[:, j].indirect(offs_t[:, e * C // 16 : (e + 1) * C // 16]),
+                rows[:, place[j] * WINDOW : (place[j] + 2) * WINDOW].indirect(offs_t[:, e * C // 16 : (e + 1) * C // 16]),
                 COPY,
             )
 
@@ -126,10 +134,10 @@ def tile_moe_shr_lin_silu_kernel(tc, xT, w_words, w_scales, b, gate, offs, pos1,
                 in_=picked[i][:, s0:s1].rearrange("p s j -> p (s j)"),
             )
 
-        cast(nc.vector.tensor_copy, 0, 0, 256)
-        cast(nc.scalar.copy, 0, 256, T)
+        cast(nc.vector.tensor_copy, 0, 0, T)
+        nc.scalar.copy(row_of[:, 0:4:2, 0:T], raw[:, 0:2])
         cast(nc.scalar.copy, 1, 0, T)
-        nc.scalar.copy(rows[:, :, 0:T], raw[:])
+        nc.scalar.copy(row_of[:, 1:4:2, 0:T], raw[:, 2:4])
         for i in range(2):
             pick_pairs(i, 0)
         for j in range(4):

import concourse.mybir as mybir
from contextlib import ExitStack

K, T, E, C, N = 512, 384, 6, 128, 512
S = E * C
P = 128
M_TILES = N // P

F32 = mybir.dt.float32
BF16 = mybir.dt.bfloat16
I32 = mybir.dt.int32
U32 = mybir.dt.uint32
U16 = mybir.dt.uint16
U8 = mybir.dt.uint8
FP8X4 = mybir.dt.float8_e4m3fn_x4
FP4X4 = mybir.dt.float4_e2m1fn_x4

MULT = mybir.AluOpType.mult
ADD = mybir.AluOpType.add
SILU = mybir.ActivationFunctionType.Silu
COPY = mybir.ActivationFunctionType.Copy

FLOPS = 2 * K * N * (S + T)
BYTES = 4 * K * T + (E + 1) * (K * N // 2 + K * N // 32) + 4 * N * (E + 1) + 2 * 4 * T + 2 * 128 * (48 + 24 + 24) + 4 * N * T

WINDOW = 512


def tile_moe_shr_lin_silu_kernel(tc, xT, w_words, w_scales, b, gate, offs, pos1, pos2, out):
    nc = tc.nc
    with ExitStack() as ctx:
        lists = ctx.enter_context(tc.tile_pool(name="lists", bufs=1))
        keep = ctx.enter_context(tc.tile_pool(name="keep", bufs=1))
        psum = ctx.enter_context(tc.psum_pool(name="psum", bufs=8))

        offs_t = lists.tile([P, S // 16], U16, name="offs_t")
        pos1_t = lists.tile([P, T // 16], U16, name="pos1_t")
        pos2_t = lists.tile([P, T // 16], U16, name="pos2_t")

        raw = keep.tile([P, 4, T], F32, name="raw")
        pairs = [keep.tile([P, 2 * WINDOW], BF16, name=f"pairs{u}", align_bytes=64) for u in range(2)]
        rows = keep.tile([P, 5 * WINDOW], BF16, name="rows", align_bytes=64)
        words = [keep.tile([P, (E + 1) * N], U8, name=f"words{h}", align_bytes=64) for h in range(2)]
        scales_w = [keep.tile([P, (E + 1) * N // 2], U8, name=f"scales_w{h}", align_bytes=64) for h in range(2)]
        bias = keep.tile([P, M_TILES, E + 1], F32, name="bias")
        dummy = keep.tile([P, 1], F32, name="dummy")
        gates = [keep.tile([P, 2, T], F32, name=f"gates{m}") for m in range(M_TILES)]

        x_rows = xT.rearrange("(p j) t -> p j t", j=4)
        nc.sync.dma_start(raw[:, 0:2], x_rows[:, 0:2])
        nc.sync.dma_start(offs_t[:], offs)
        nc.sync.dma_start(raw[:, 2:4], x_rows[:, 2:4])

        for h in range(2):
            nc.vector.memset(scales_w[h][:].bitcast(I32), 0)
        nc.gpsimd.memset(dummy[:], 0.0)
        nc.scalar.activation(dummy[:], dummy[:], SILU)
        for u in range(2):
            nc.gpsimd.memset(pairs[u][:, 2 * T :], 0.0)
        row_of = rows[:].rearrange("p (r t) -> p r t", t=WINDOW)
        nc.gpsimd.memset(row_of[:, 0:4, T:], 0.0)
        nc.gpsimd.memset(row_of[:, 4], 0.0)
        place = (0, 2, 1, 3)

        w_scales_i = w_scales.bitcast(I32)
        w_i = w_words.bitcast(I32)

        def load_weights(h):
            nc.sync.dma_start(
                words[h][:].bitcast(I32).rearrange("p (e c) -> p e c", e=E + 1),
                w_i[:, 0, :, h * N // 4 : (h + 1) * N // 4].rearrange("e p c -> p e c"),
            )
            for q in range(4):
                nc.sync.dma_start(
                    scales_w[h][:].bitcast(I32).rearrange("p (e c) -> p e c", e=E + 1)[32 * q : 32 * q + 4],
                    w_scales_i[:, 0, 4 * q : 4 * q + 4, h * N // 8 : (h + 1) * N // 8].rearrange("e q c -> q e c"),
                )

        def load_gates(m):
            nc.sync.dma_start(gates[m][:], gate[:, m * P : (m + 1) * P, :].rearrange("r p t -> p r t"))

        load_weights(0)
        nc.sync.dma_start(bias[:], b.rearrange("(m p) e -> p m e", p=P))
        load_gates(0)
        nc.sync.dma_start(pos1_t[:], pos1)
        nc.sync.dma_start(pos2_t[:], pos2)
        load_weights(1)
        for m in range(1, M_TILES):
            load_gates(m)

        def cast(engine_copy, u, t0, t1):
            engine_copy(
                pairs[u][:, 2 * t0 : 2 * t1].rearrange("p (t e) -> p t e", e=2),
                raw[:, 2 * u : 2 * u + 2, t0:t1].rearrange("p e t -> p t e"),
            )

        def lhsT(e, m):
            col = e * N // 2 + m % 2 * P
            return dict(
                lhsT=words[m // 2][:, 2 * col : 2 * (col + P)].bitcast(FP4X4),
                lhsT_scale=scales_w[m // 2][:, col : col + P],
            )

        windows = [pairs[u][:].bitcast(U32) for u in range(2)]
        spans = ((0, 5 * C), (5 * C, S), (S, S + T))
        picked = [keep.tile([P, s1 - s0, 4], BF16, name=f"picked{s0}", align_bytes=64) for s0, s1 in spans]
        codes = [keep.tile([P, s1 - s0], U32, name=f"codes{s0}", align_bytes=64) for s0, s1 in spans]
        scales = [keep.tile([P, s1 - s0], U8, name=f"scales{s0}", align_bytes=64) for s0, s1 in spans]
        CUTS = ((0, 384), (384, 640))
        planes = [keep.tile([P, 2, 2 * (s1 - s0)], BF16, name=f"planes{s0}", align_bytes=64) for s0, s1 in CUTS]

        def pick_pairs(i, u):
            s0, s1 = CUTS[i]
            nc.vector.tensor_copy(planes[i][:, u].bitcast(U32), windows[u].indirect(offs_t[:, s0 // 16 : s1 // 16]))

        def interleave(i):
            s0, s1 = CUTS[i]
            nc.vector.tensor_copy(
                picked[0][:, s0:s1].rearrange("p s j -> p (s j)").bitcast(I32).rearrange("p (s u) -> p s u", u=2),
                planes[i][:].rearrange("p u c -> p (u c)").bitcast(I32).rearrange("p (u s) -> p s u", u=2),
            )

        def pick_row(e, j):
            nc.scalar.activation(
                picked[1][:, :, j],
                rows[:, place[j] * WINDOW : (place[j] + 2) * WINDOW].indirect(offs_t[:, e * C // 16 : (e + 1) * C // 16]),
                COPY,
            )

        def quantise(i, s0, s1):
            nc.vector.quantize_mx(
                out=codes[i][:, s0:s1].bitcast(FP8X4),
                scales=scales[i][:, s0:s1],
                in_=picked[i][:, s0:s1].rearrange("p s j -> p (s j)"),
            )

        cast(nc.vector.tensor_copy, 0, 0, T)
        nc.scalar.copy(row_of[:, 0:4:2, 0:T], raw[:, 0:2])
        cast(nc.scalar.copy, 1, 0, T)
        nc.scalar.copy(row_of[:, 1:4:2, 0:T], raw[:, 2:4])
        for i in range(2):
            pick_pairs(i, 0)
        for j in range(4):
            pick_row(5, j)
        for t0, t1 in ((0, 128), (128, 256), (256, T)):
            nc.gpsimd.tensor_scalar(
                picked[2][:, t0:t1], raw[:, :, t0:t1].rearrange("p j t -> p t j"), 1.0, 0.0, MULT, ADD
            )
        for i in range(2):
            pick_pairs(i, 1)
        for i in range(2):
            interleave(i)
        for i, s0, s1 in ((0, 0, 256), (0, 256, 512), (0, 512, 640), (1, 0, 128), (2, 0, 256), (2, 256, 384)):
            quantise(i, s0, s1)

        y = [keep.tile([P, S], F32, name=f"y{m}") for m in range(M_TILES)]
        ys = [keep.tile([P, 2, T], F32, name=f"ys{m}") for m in range(2)]

        def product(sums, e, m, s0, s1):
            i = [j for j in range(3) if spans[j][0] <= s0 < spans[j][1]][0]
            s0, s1 = s0 - spans[i][0], s1 - spans[i][0]
            nc.tensor.matmul_mx(
                out=sums,
                rhs=codes[i][:, s0:s1].bitcast(FP8X4),
                rhs_scale=scales[i][:, s0:s1],
                start=True,
                stop=True,
                **lhsT(e, m),
            )

        for m in range(M_TILES):
            for e0 in (0, 2, 4):
                sums = psum.tile([P, 2, C], F32, name="sums")
                for e in (e0, e0 + 1):
                    product(sums[:, e - e0], e, m, e * C, (e + 1) * C)
                for e in (e0, e0 + 1):
                    nc.scalar.activation(
                        y[m][:, e * C : (e + 1) * C], sums[:, e - e0], SILU, bias=bias[:, m, e : e + 1]
                    )
            sums = psum.tile([P, T], F32, name="sums")
            for t0, t1 in ((0, 256), (256, T)):
                product(sums[:, t0:t1], E, m, S + t0, S + t1)
            nc.scalar.activation(ys[m // 2][:, m % 2], sums[:], SILU, bias=bias[:, m, E : E + 1])

        first = [keep.tile([P, 2, T], F32, name=f"first{m}") for m in range(2)]
        second = [keep.tile([P, 2, T], F32, name=f"second{m}") for m in range(2)]
        part = [keep.tile([P, 2, T], F32, name=f"part{m}") for m in range(2)]
        total = [keep.tile([P, 2, T], F32, name=f"total{m}") for m in range(2)]

        def gather(to, m, listed, r, t0=0, t1=T):
            nc.vector.tensor_tensor(
                to[m // 2][:, m % 2, t0:t1],
                y[m][:].indirect(listed[:, t0 // 16 : t1 // 16]),
                gates[m][:, r, t0:t1],
                MULT,
            )

        def add(to, a, b, m, span, t0=0, t1=T):
            at = (slice(None), slice(m % 2, m % 2 + span), slice(t0, t1))
            nc.vector.tensor_tensor(to[m // 2][at], a[m // 2][at], b[m // 2][at], ADD)

        def store(m, t0=0, t1=T):
            nc.sync.dma_start(out[m * P : (m + 1) * P, t0:t1], total[m // 2][:, m % 2, t0:t1])

        gather(first, 0, pos1_t, 0)
        gather(second, 0, pos2_t, 1)
        gather(first, 1, pos1_t, 0)
        gather(second, 1, pos2_t, 1)
        add(part, ys, first, 0, 2)
        gather(first, 2, pos1_t, 0)
        add(total, part, second, 0, 2)
        store(0)
        store(1)
        gather(second, 2, pos2_t, 1)
        add(part, ys, first, 2, 1)
        gather(first, 3, pos1_t, 0)
        add(total, part, second, 2, 1)
        store(2)
        LATE = 256
        gather(second, 3, pos2_t, 1, 0, LATE)
        add(part, ys, first, 3, 1)
        gather(second, 3, pos2_t, 1, LATE, T)
        add(total, part, second, 3, 1, 0, LATE)
        store(3, 0, LATE)
        add(total, part, second, 3, 1, LATE, T)
        store(3, LATE, T)
